import numpy as np
import ml_dtypes


def mxq(x, axis, fmt="e4m3"):
    dtype, down = {"e4m3": (ml_dtypes.float8_e4m3fn, 7), "e5m2": (ml_dtypes.float8_e5m2, 14)}[fmt]
    v = np.moveaxis(np.asarray(x, np.float32).astype(ml_dtypes.bfloat16).astype(np.float64), axis, -1)
    blocks = v.reshape(v.shape[:-1] + (-1, 32))
    amax = np.abs(blocks).max(-1, keepdims=True)
    byte = np.maximum(np.where(amax > 0, np.frexp(amax)[1] - 1 + 127, 0) - down, 1)
    scale = np.exp2(byte - 127.0)
    codes = (blocks / scale).astype(np.float32).astype(dtype).astype(np.float64)
    return np.moveaxis((codes * scale).reshape(v.shape), -1, axis)


WIDE = False


def mx_kscale(k):
    if not WIDE:
        return np.ones(k)
    levels = np.array([10, -10, 5, -5, 0])
    if k % 512:
        return np.exp2(np.random.permutation(np.resize(levels, k // 32))).repeat(32)
    a = np.empty((k // 512, 16))
    for p in range(k // 512):
        a[p, :8] = np.random.permutation(np.resize(levels, 8))
        for g in range(8):
            far = levels[np.abs(levels - a[p, g]) >= 10]
            a[p, g + 8] = far[np.random.randint(len(far))]
    return np.exp2(a.ravel()).repeat(32)


def f64(x):
    return np.asarray(x).astype(np.float64)


def striped(idx):
    return np.tile(idx.reshape(-1, 16).T, (8, 1)).astype(np.uint16)


def unstriped(offs):
    return offs[:16].T.reshape(-1).astype(np.int64)


E2M1 = np.array([0.0, 0.5, 1.0, 1.5, 2.0, 3.0, 4.0, 6.0, -0.0, -0.5, -1.0, -1.5, -2.0, -3.0, -4.0, -6.0])


def pack_weight(w, fmt):
    k, n = w.shape
    w = f64(np.asarray(w, np.float32).astype(ml_dtypes.bfloat16)).reshape(k // 32, 32, n)
    amax = np.abs(w).max(1)
    if fmt == "e4m3":
        byte = np.frexp(amax)[1] - 1 + 127 - 7
    else:
        mant, ex = np.frexp(amax / 6.0)
        byte = np.where(mant > 0.5, ex, ex - 1) + 127
    byte = np.clip(np.where(amax > 0, byte, 1), 1, 254)
    scaled = (w * np.exp2(127.0 - byte)[:, None, :]).reshape(k, n).astype(np.float32)
    by_word = np.ascontiguousarray(scaled.reshape(k // 512, 128, 4, n).transpose(0, 1, 3, 2))
    if fmt == "e4m3":
        words = by_word.astype(ml_dtypes.float8_e4m3fn).view(np.uint8)
    else:
        c = by_word.astype(ml_dtypes.float4_e2m1fn).view(np.uint8) & 0xF
        words = (c[..., 0::2] | (c[..., 1::2] << 4)).reshape(k // 512, 128, 2 * n)
    return np.ascontiguousarray(words), np.ascontiguousarray(byte.astype(np.uint8).reshape(k // 512, 16, n))


def unpack_weight(words, scales, fmt):
    g, _, n = scales.shape
    words = np.ascontiguousarray(words).reshape(g, 128, n, -1)
    if fmt == "e4m3":
        vals = words.view(ml_dtypes.float8_e4m3fn).astype(np.float64)
    else:
        nib = np.empty((g, 128, n, 4), np.uint8)
        nib[..., 0::2] = words & 0xF
        nib[..., 1::2] = words >> 4
        vals = E2M1[nib]
    vals = vals * np.repeat(np.exp2(scales.astype(np.float64) - 127.0), 8, axis=1)[..., None]
    return vals.transpose(0, 1, 3, 2).reshape(g * 512, n)


def pack_table(v):
    words, scales = pack_weight(v, "e4m3")
    return np.concatenate([words.reshape(words.shape[0], -1), scales.reshape(scales.shape[0], -1)], axis=1)


def unpack_table(tab):
    g, t = tab.shape[0], tab.shape[1] // 528
    return unpack_weight(tab[:, :512 * t].reshape(g, 128, t, 4), tab[:, 512 * t:].reshape(g, 16, t), "e4m3")


def split(x):
    m, e = np.frexp(f64(x))
    hi = np.ldexp(np.trunc(16.0 * m) / 16.0, e)
    return hi, f64(x) - hi


K, M, T, S = 1024, 512, 1024, 512


def setup_inputs():
    n = np.random.standard_normal
    s = mx_kscale(K)[:, None]
    return {
        "tab": pack_table(n((K, T)) * s),
        "w": (n((K, M)) / np.sqrt(K) / s).astype(np.float32),
        "b": (0.3 * n(512)).astype(np.float32),
        "offs": striped(np.random.permutation(T)[:S]),
    }


def reference(tab, w, b, offs):
    tab_ = unpack_table(tab)[:, unstriped(offs)]
    w_hi, w_lo = split(w)
    w_hi_, w_lo_ = mxq(w_hi, 0, "e4m3"), mxq(w_lo, 0, "e4m3")
    y = w_hi_.T @ tab_ + w_lo_.T @ tab_
    return y + f64(b)[:, None]

@@ -1,0 +1,181 @@
+import concourse.mybir as mybir
+
+K, M, T, S = 1024, 512, 1024, 512
+FLOPS = 2 * 2 * K * M * S
+
+F32 = mybir.dt.float32
+BF16 = mybir.dt.bfloat16
+I32 = mybir.dt.int32
+U32 = mybir.dt.uint32
+U16 = mybir.dt.uint16
+U8 = mybir.dt.uint8
+FP8X4 = mybir.dt.float8_e4m3fn_x4
+ALU = mybir.AluOpType
+ACT = mybir.ActivationFunctionType
+
+P = 128
+PACK = 4
+K_PASS = P * PACK
+MASK = -983056
+
+
+def tile_list_tabw_hl_bias_kernel(tc, tab, w, b, offs, out):
+    nc = tc.nc
+    with (
+        tc.tile_pool(name="keep", bufs=1) as keep,
+        tc.psum_pool(name="psum", bufs=1) as psum,
+    ):
+        offsets = keep.tile([P, S // 16], U16, name="offsets")
+        planes = keep.tile([P, T // 4], I32, name="planes", align_bytes=64)
+        bias = keep.tile([P, M // P], F32, name="bias")
+        dummy = keep.tile([P, 1], F32, name="dummy")
+        nc.gpsimd.memset(planes[:], 0)
+        nc.vector.memset(dummy[:], 0.0)
+
+        nc.sync.dma_start(offsets[:], offs)
+        for q in range(4):
+            lo = 4 * P * T + 4 * q * T
+            nc.sync.dma_start(
+                out=planes[32 * q : 32 * q + 8, :],
+                in_=tab[:, lo : lo + 4 * T].rearrange("a (r t) -> a r t", r=4).bitcast(I32),
+            )
+        nc.scalar.activation(dummy[:], dummy[:], ACT.Identity)
+
+        units = [(0, 0, 128), (0, 128, 128), (1, 0, 256), (0, 256, 256), (1, 256, 128), (1, 384, 128)]
+        w_sb, top, hl, codes, scales = [], [], [], [], []
+        for u, (a, c, n) in enumerate(units):
+            w_sb.append(keep.tile([P, PACK, n], F32, name="w_sb%d" % u, align_bytes=64))
+            top.append(keep.tile([P, n, PACK], BF16, name="top%d" % u, align_bytes=64))
+            hl.append(keep.tile([P, 2, n, PACK], BF16, name="hl%d" % u, align_bytes=64))
+            codes.append(keep.tile([P, 2, n], U32, name="codes%d" % u, align_bytes=64))
+            scales.append(keep.tile([P, 2, n], U8, name="scales%d" % u, align_bytes=64))
+        words = [keep.tile([P, T], I32, name="words%d" % a, align_bytes=64) for a in range(2)]
+        picked = [keep.tile([P, S], U32, name="picked%d" % a, align_bytes=64) for a in range(2)]
+        picked_scales = keep.tile([P, S], U8, name="picked_scales", align_bytes=64)
+
+        def load_w(u):
+            a, c, n = units[u]
+            nc.sync.dma_start(
+                out=w_sb[u][:],
+                in_=w[a * K_PASS : (a + 1) * K_PASS, c : c + n].rearrange("(p j) n -> p j n", j=PACK),
+            )
+
+        def load_table(a):
+            nc.sync.dma_start(
+                out=words[a][:],
+                in_=tab[a, 0 : 4 * P * T].rearrange("(p x) -> p x", p=P).bitcast(I32),
+            )
+
+        load_w(0)
+        load_table(0)
+        load_w(1)
+        load_table(1)
+        for u in range(2, len(units)):
+            load_w(u)
+
+        with nc.allow_non_contiguous_dma(reason="512 bias values, one to a partition and column"):
+            nc.sync.dma_start(out=bias[:], in_=b.rearrange("(m p) -> p m", p=P))
+
+        def take_top(u):
+            upper = w_sb[u][:].bitcast(BF16).rearrange("p j (c i e) -> p c j i e", i=4, e=2)[:, :, :, :, 1]
+            nc.scalar.copy(out=top[u][:].rearrange("p (c i) j -> p c j i", i=4), in_=upper)
+
+        def mask(u):
+            nc.vector.tensor_scalar(
+                hl[u][:, 0].rearrange("p n j -> p (n j)").bitcast(I32),
+                top[u][:].rearrange("p n j -> p (n j)").bitcast(I32),
+                MASK,
+                None,
+                op0=ALU.bitwise_and,
+            )
+
+        def rest(u):
+            nc.vector.tensor_tensor(
+                out=hl[u][:, 1].rearrange("p (c i) j -> p c j i", i=4),
+                in0=w_sb[u][:].rearrange("p j (c i) -> p c j i", i=4),
+                in1=hl[u][:, 0].rearrange("p (c i) j -> p c j i", i=4),
+                op=ALU.subtract,
+            )
+
+        def quantize(u, parts=slice(0, 2)):
+            nc.vector.quantize_mx(
+                out=codes[u][:, parts].rearrange("p s n -> p (s n)").bitcast(FP8X4),
+                scales=scales[u][:, parts].rearrange("p s n -> p (s n)"),
+                in_=hl[u][:, parts].rearrange("p s n j -> p (s n j)"),
+            )
+
+        def gather_words(a):
+            nc.vector.tensor_copy(picked[a][:], words[a][:].bitcast(U32).indirect(offsets[:]))
+
+        banks = {}
+        for m in range(4):
+            halves = [(0, 512)] if m < 2 else [(0, 256), (256, 256)]
+            banks[m] = [(j0, jn, psum.tile([P, 512], F32, name="acc%d_%d" % (m, j0))) for j0, jn in halves]
+
+        def multiply(u, part):
+            a, c, n = units[u]
+            for m in range(c // P, (c + n) // P):
+                cols = slice(m * P - c, m * P - c + P)
+                for j0, jn, acc in banks[m]:
+                    nc.tensor.matmul_mx(
+                        out=acc[:, 0:jn],
+                        lhsT=codes[u][:, part, cols].bitcast(FP8X4),
+                        lhsT_scale=scales[u][:, part, cols],
+                        rhs=picked[a][:, j0 : j0 + jn].bitcast(FP8X4),
+                        rhs_scale=picked_scales[4 * a : P, j0 : j0 + jn],
+                        start=(a == 0 and part == 0),
+                        stop=(a == 1 and part == 1),
+                    )
+
+        def finish(m, h, engine):
+            j0, jn, acc = banks[m][h]
+            res = keep.tile([P, jn], F32, name="res%d_%d" % (m, j0), align_bytes=64)
+            if engine == "scalar":
+                nc.scalar.activation(res[:], acc[:, 0:jn], ACT.Identity, bias=bias[:, m : m + 1])
+            else:
+                nc.vector.tensor_scalar(res[:], acc[:, 0:jn], bias[:, m : m + 1], None, op0=ALU.add)
+            nc.sync.dma_start(out=out[m * P : (m + 1) * P, j0 : j0 + jn], in_=res[:])
+
+        for u in range(len(units)):
+            take_top(u)
+
+        nc.vector.tensor_copy(picked_scales[:], planes[:].bitcast(U8).indirect(offsets[:]))
+        mask(0)
+        rest(0)
+        gather_words(0)
+        quantize(0)
+        mask(1)
+        rest(1)
+        multiply(0, 0)
+        multiply(0, 1)
+        gather_words(1)
+        quantize(1)
+        multiply(1, 0)
+        multiply(1, 1)
+        mask(2)
+        rest(2)
+        mask(3)
+        quantize(2)
+        multiply(2, 0)
+        multiply(2, 1)
+        finish(0, 0, "scalar")
+        finish(1, 0, "scalar")
+        rest(3)
+        mask(4)
+        quantize(3)
+        multiply(3, 0)
+        multiply(3, 1)
+        mask(5)
+        rest(4)
+        quantize(5, slice(0, 1))
+        multiply(5, 0)
+        rest(5)
+        quantize(4)
+        multiply(4, 0)
+        multiply(4, 1)
+        quantize(5, slice(1, 2))
+        multiply(5, 1)
+        finish(2, 0, "vector")
+        finish(2, 1, "scalar")
+        finish(3, 0, "vector")
+        finish(3, 1, "scalar")

@@ -89,8 +89,8 @@ def tile_list_tabw_hl_bias_kernel(tc, tab, w, b, offs, out):
                 op0=ALU.bitwise_and,
             )
 
-        def rest(u):
-            nc.vector.tensor_tensor(
+        def rest(u, engine=nc.vector):
+            engine.tensor_tensor(
                 out=hl[u][:, 1].rearrange("p (c i) j -> p c j i", i=4),
                 in0=w_sb[u][:].rearrange("p j (c i) -> p c j i", i=4),
                 in1=hl[u][:, 0].rearrange("p (c i) j -> p c j i", i=4),
@@ -141,18 +141,18 @@ def tile_list_tabw_hl_bias_kernel(tc, tab, w, b, offs, out):
 
         nc.vector.tensor_copy(picked_scales[:], planes[:].bitcast(U8).indirect(offsets[:]))
         mask(0)
-        rest(0)
         gather_words(0)
-        quantize(0)
+        rest(0, nc.gpsimd)
         mask(1)
-        rest(1)
+        quantize(0)
         multiply(0, 0)
         multiply(0, 1)
         gather_words(1)
+        rest(1, nc.gpsimd)
+        mask(2)
         quantize(1)
         multiply(1, 0)
         multiply(1, 1)
-        mask(2)
         rest(2)
         mask(3)
         quantize(2)

@@ -31,17 +31,9 @@ def tile_list_tabw_hl_bias_kernel(tc, tab, w, b, offs, out):
         dummy = keep.tile([P, 1], F32, name="dummy")
         nc.gpsimd.memset(planes[:], 0)
         nc.vector.memset(dummy[:], 0.0)
-
-        nc.sync.dma_start(offsets[:], offs)
-        for q in range(4):
-            lo = 4 * P * T + 4 * q * T
-            nc.sync.dma_start(
-                out=planes[32 * q : 32 * q + 8, :],
-                in_=tab[:, lo : lo + 4 * T].rearrange("a (r t) -> a r t", r=4).bitcast(I32),
-            )
         nc.scalar.activation(dummy[:], dummy[:], ACT.Identity)
 
-        units = [(0, 0, 128), (0, 128, 128), (1, 0, 256), (0, 256, 256), (1, 256, 128), (1, 384, 128)]
+        units = [(0, 0, 256), (1, 0, 256), (0, 256, 256), (1, 256, 256)]
         w_sb, top, hl, codes, scales = [], [], [], [], []
         for u, (a, c, n) in enumerate(units):
             w_sb.append(keep.tile([P, PACK, n], F32, name="w_sb%d" % u, align_bytes=64))
@@ -66,66 +58,80 @@ def tile_list_tabw_hl_bias_kernel(tc, tab, w, b, offs, out):
                 in_=tab[a, 0 : 4 * P * T].rearrange("(p x) -> p x", p=P).bitcast(I32),
             )
 
-        load_w(0)
-        load_table(0)
-        load_w(1)
-        load_table(1)
-        for u in range(2, len(units)):
-            load_w(u)
+        def load_offsets():
+            nc.sync.dma_start(offsets[:], offs)
 
-        with nc.allow_non_contiguous_dma(reason="512 bias values, one to a partition and column"):
-            nc.sync.dma_start(out=bias[:], in_=b.rearrange("(m p) -> p m", p=P))
+        def load_rows():
+            for q in range(4):
+                lo = 4 * P * T + 4 * q * T
+                nc.sync.dma_start(
+                    out=planes[32 * q : 32 * q + 8, :],
+                    in_=tab[:, lo : lo + 4 * T].rearrange("a (r t) -> a r t", r=4).bitcast(I32),
+                )
 
-        def take_top(u):
-            upper = w_sb[u][:].bitcast(BF16).rearrange("p j (c i e) -> p c j i e", i=4, e=2)[:, :, :, :, 1]
-            nc.scalar.copy(out=top[u][:].rearrange("p (c i) j -> p c j i", i=4), in_=upper)
+        def load_bias():
+            with nc.allow_non_contiguous_dma(reason="512 bias values, one to a partition and column"):
+                nc.sync.dma_start(out=bias[:], in_=b.rearrange("(m p) -> p m", p=P))
 
-        def mask(u):
+        def take_top(u, c0, n):
+            upper = w_sb[u][:, :, c0 : c0 + n].bitcast(BF16).rearrange("p j (c i e) -> p c j i e", i=4, e=2)[:, :, :, :, 1]
+            nc.scalar.copy(out=top[u][:, c0 : c0 + n].rearrange("p (c i) j -> p c j i", i=4), in_=upper)
+
+        def mask(u, c0, n):
             nc.vector.tensor_scalar(
-                hl[u][:, 0].rearrange("p n j -> p (n j)").bitcast(I32),
-                top[u][:].rearrange("p n j -> p (n j)").bitcast(I32),
+                hl[u][:, 0, c0 : c0 + n].rearrange("p n j -> p (n j)").bitcast(I32),
+                top[u][:, c0 : c0 + n].rearrange("p n j -> p (n j)").bitcast(I32),
                 MASK,
                 None,
                 op0=ALU.bitwise_and,
             )
 
-        def rest(u, engine=nc.vector):
+        def rest(u, c0, n, engine=nc.vector):
             engine.tensor_tensor(
-                out=hl[u][:, 1].rearrange("p (c i) j -> p c j i", i=4),
-                in0=w_sb[u][:].rearrange("p j (c i) -> p c j i", i=4),
-                in1=hl[u][:, 0].rearrange("p (c i) j -> p c j i", i=4),
+                out=hl[u][:, 1, c0 : c0 + n].rearrange("p (c i) j -> p c j i", i=4),
+                in0=w_sb[u][:, :, c0 : c0 + n].rearrange("p j (c i) -> p c j i", i=4),
+                in1=hl[u][:, 0, c0 : c0 + n].rearrange("p (c i) j -> p c j i", i=4),
                 op=ALU.subtract,
             )
 
-        def quantize(u, parts=slice(0, 2)):
+        def quantize_both(u):
             nc.vector.quantize_mx(
-                out=codes[u][:, parts].rearrange("p s n -> p (s n)").bitcast(FP8X4),
-                scales=scales[u][:, parts].rearrange("p s n -> p (s n)"),
-                in_=hl[u][:, parts].rearrange("p s n j -> p (s n j)"),
+                out=codes[u][:].rearrange("p s n -> p (s n)").bitcast(FP8X4),
+                scales=scales[u][:].rearrange("p s n -> p (s n)"),
+                in_=hl[u][:].rearrange("p s n j -> p (s n j)"),
+            )
+
+        def quantize_part(u, s, c0, n):
+            nc.vector.quantize_mx(
+                out=codes[u][:, s, c0 : c0 + n].bitcast(FP8X4),
+                scales=scales[u][:, s, c0 : c0 + n],
+                in_=hl[u][:, s, c0 : c0 + n].rearrange("p n j -> p (n j)"),
             )
 
         def gather_words(a):
             nc.vector.tensor_copy(picked[a][:], words[a][:].bitcast(U32).indirect(offsets[:]))
+
+        def gather_scales():
+            nc.vector.tensor_copy(picked_scales[:], planes[:].bitcast(U8).indirect(offsets[:]))
 
         banks = {}
         for m in range(4):
             halves = [(0, 512)] if m < 2 else [(0, 256), (256, 256)]
             banks[m] = [(j0, jn, psum.tile([P, 512], F32, name="acc%d_%d" % (m, j0))) for j0, jn in halves]
 
-        def multiply(u, part):
+        def multiply(u, part, m):
             a, c, n = units[u]
-            for m in range(c // P, (c + n) // P):
-                cols = slice(m * P - c, m * P - c + P)
-                for j0, jn, acc in banks[m]:
-                    nc.tensor.matmul_mx(
-                        out=acc[:, 0:jn],
-                        lhsT=codes[u][:, part, cols].bitcast(FP8X4),
-                        lhsT_scale=scales[u][:, part, cols],
-                        rhs=picked[a][:, j0 : j0 + jn].bitcast(FP8X4),
-                        rhs_scale=picked_scales[4 * a : P, j0 : j0 + jn],
-                        start=(a == 0 and part == 0),
-                        stop=(a == 1 and part == 1),
-                    )
+            cols = slice(m * P - c, m * P - c + P)
+            for j0, jn, acc in banks[m]:
+                nc.tensor.matmul_mx(
+                    out=acc[:, 0:jn],
+                    lhsT=codes[u][:, part, cols].bitcast(FP8X4),
+                    lhsT_scale=scales[u][:, part, cols],
+                    rhs=picked[a][:, j0 : j0 + jn].bitcast(FP8X4),
+                    rhs_scale=picked_scales[4 * a : P, j0 : j0 + jn],
+                    start=(a == 0 and part == 0),
+                    stop=(a == 1 and part == 1),
+                )
 
         def finish(m, h, engine):
             j0, jn, acc = banks[m][h]
@@ -136,45 +142,57 @@ def tile_list_tabw_hl_bias_kernel(tc, tab, w, b, offs, out):
                 nc.vector.tensor_scalar(res[:], acc[:, 0:jn], bias[:, m : m + 1], None, op0=ALU.add)
             nc.sync.dma_start(out=out[m * P : (m + 1) * P, j0 : j0 + jn], in_=res[:])
 
-        for u in range(len(units)):
-            take_top(u)
-
-        nc.vector.tensor_copy(picked_scales[:], planes[:].bitcast(U8).indirect(offsets[:]))
-        mask(0)
+        load_table(0)
+        load_offsets()
+        load_table(1)
+        load_rows()
+        load_w(0)
+        load_w(1)
+        load_w(2)
+        load_w(3)
+        load_bias()
+        take_top(0, 0, 128)
+        take_top(0, 128, 128)
+        take_top(1, 0, 128)
+        take_top(1, 128, 128)
+        take_top(2, 0, 256)
+        take_top(3, 0, 256)
         gather_words(0)
-        rest(0, nc.gpsimd)
-        mask(1)
-        quantize(0)
-        multiply(0, 0)
-        multiply(0, 1)
         gather_words(1)
-        rest(1, nc.gpsimd)
-        mask(2)
-        quantize(1)
-        multiply(1, 0)
-        multiply(1, 1)
-        rest(2)
-        mask(3)
-        quantize(2)
-        multiply(2, 0)
-        multiply(2, 1)
+        gather_scales()
+        mask(0, 0, 256)
+        rest(0, 0, 256)
+        mask(1, 0, 256)
+        quantize_both(0)
+        multiply(0, 0, 0)
+        multiply(0, 1, 0)
+        multiply(0, 0, 1)
+        multiply(0, 1, 1)
+        rest(1, 0, 256)
+        mask(2, 0, 256)
+        quantize_both(1)
+        multiply(1, 0, 0)
+        multiply(1, 1, 0)
         finish(0, 0, "scalar")
+        multiply(1, 0, 1)
+        multiply(1, 1, 1)
         finish(1, 0, "scalar")
-        rest(3)
-        mask(4)
-        quantize(3)
-        multiply(3, 0)
-        multiply(3, 1)
-        mask(5)
-        rest(4)
-        quantize(5, slice(0, 1))
-        multiply(5, 0)
-        rest(5)
-        quantize(4)
-        multiply(4, 0)
-        multiply(4, 1)
-        quantize(5, slice(1, 2))
-        multiply(5, 1)
+        rest(2, 0, 256)
+        mask(3, 0, 256)
+        quantize_both(2)
+        multiply(2, 0, 2)
+        multiply(2, 1, 2)
+        multiply(2, 0, 3)
+        multiply(2, 1, 3)
+        rest(3, 0, 128)
+        quantize_part(3, 0, 0, 256)
+        multiply(3, 0, 2)
+        multiply(3, 0, 3)
+        rest(3, 128, 128)
+        quantize_part(3, 1, 0, 128)
+        multiply(3, 1, 2)
+        quantize_part(3, 1, 128, 128)
+        multiply(3, 1, 3)
         finish(2, 0, "vector")
         finish(2, 1, "scalar")
         finish(3, 0, "vector")

import concourse.mybir as mybir

K, M, T, S = 1024, 512, 1024, 512
FLOPS = 2 * 2 * K * M * S

F32 = mybir.dt.float32
BF16 = mybir.dt.bfloat16
I32 = mybir.dt.int32
U32 = mybir.dt.uint32
U16 = mybir.dt.uint16
U8 = mybir.dt.uint8
FP8X4 = mybir.dt.float8_e4m3fn_x4
ALU = mybir.AluOpType
ACT = mybir.ActivationFunctionType

P = 128
PACK = 4
K_PASS = P * PACK
MASK = -983056


def tile_list_tabw_hl_bias_kernel(tc, tab, w, b, offs, out):
    nc = tc.nc
    with (
        tc.tile_pool(name="keep", bufs=1) as keep,
        tc.psum_pool(name="psum", bufs=1) as psum,
    ):
        offsets = keep.tile([P, S // 16], U16, name="offsets")
        planes = keep.tile([P, T // 4], I32, name="planes", align_bytes=64)
        bias = keep.tile([P, M // P], F32, name="bias")
        dummy = keep.tile([P, 1], F32, name="dummy")
        nc.gpsimd.memset(planes[:], 0)
        nc.vector.memset(dummy[:], 0.0)
        nc.scalar.activation(dummy[:], dummy[:], ACT.Identity)

        units = [(0, 0, 256), (1, 0, 256), (0, 256, 256), (1, 256, 256)]
        w_sb, top, hl, codes, scales = [], [], [], [], []
        for u, (a, c, n) in enumerate(units):
            w_sb.append(keep.tile([P, PACK, n], F32, name="w_sb%d" % u, align_bytes=64))
            top.append(keep.tile([P, n, PACK], BF16, name="top%d" % u, align_bytes=64))
            hl.append(keep.tile([P, 2, n, PACK], BF16, name="hl%d" % u, align_bytes=64))
            codes.append(keep.tile([P, 2, n], U32, name="codes%d" % u, align_bytes=64))
            scales.append(keep.tile([P, 2, n], U8, name="scales%d" % u, align_bytes=64))
        words = [keep.tile([P, T], I32, name="words%d" % a, align_bytes=64) for a in range(2)]
        picked = [keep.tile([P, S], U32, name="picked%d" % a, align_bytes=64) for a in range(2)]
        picked_scales = keep.tile([P, S], U8, name="picked_scales", align_bytes=64)

        def load_w(u):
            a, c, n = units[u]
            nc.sync.dma_start(
                out=w_sb[u][:],
                in_=w[a * K_PASS : (a + 1) * K_PASS, c : c + n].rearrange("(p j) n -> p j n", j=PACK),
            )

        def load_table(a):
            nc.sync.dma_start(
                out=words[a][:],
                in_=tab[a, 0 : 4 * P * T].rearrange("(p x) -> p x", p=P).bitcast(I32),
            )

        def load_offsets():
            nc.sync.dma_start(offsets[:], offs)

        def load_rows():
            for q in range(4):
                lo = 4 * P * T + 4 * q * T
                nc.sync.dma_start(
                    out=planes[32 * q : 32 * q + 8, :],
                    in_=tab[:, lo : lo + 4 * T].rearrange("a (r t) -> a r t", r=4).bitcast(I32),
                )

        def load_bias():
            with nc.allow_non_contiguous_dma(reason="512 bias values, one to a partition and column"):
                nc.sync.dma_start(out=bias[:], in_=b.rearrange("(m p) -> p m", p=P))

        def take_top(u, c0, n):
            upper = w_sb[u][:, :, c0 : c0 + n].bitcast(BF16).rearrange("p j (c i e) -> p c j i e", i=4, e=2)[:, :, :, :, 1]
            nc.scalar.copy(out=top[u][:, c0 : c0 + n].rearrange("p (c i) j -> p c j i", i=4), in_=upper)

        def mask(u, c0, n):
            nc.vector.tensor_scalar(
                hl[u][:, 0, c0 : c0 + n].rearrange("p n j -> p (n j)").bitcast(I32),
                top[u][:, c0 : c0 + n].rearrange("p n j -> p (n j)").bitcast(I32),
                MASK,
                None,
                op0=ALU.bitwise_and,
            )

        def rest(u, c0, n, engine=nc.vector):
            engine.tensor_tensor(
                out=hl[u][:, 1, c0 : c0 + n].rearrange("p (c i) j -> p c j i", i=4),
                in0=w_sb[u][:, :, c0 : c0 + n].rearrange("p j (c i) -> p c j i", i=4),
                in1=hl[u][:, 0, c0 : c0 + n].rearrange("p (c i) j -> p c j i", i=4),
                op=ALU.subtract,
            )

        def quantize_both(u):
            nc.vector.quantize_mx(
                out=codes[u][:].rearrange("p s n -> p (s n)").bitcast(FP8X4),
                scales=scales[u][:].rearrange("p s n -> p (s n)"),
                in_=hl[u][:].rearrange("p s n j -> p (s n j)"),
            )

        def quantize_part(u, s, c0, n):
            nc.vector.quantize_mx(
                out=codes[u][:, s, c0 : c0 + n].bitcast(FP8X4),
                scales=scales[u][:, s, c0 : c0 + n],
                in_=hl[u][:, s, c0 : c0 + n].rearrange("p n j -> p (n j)"),
            )

        def gather_words(a):
            nc.vector.tensor_copy(picked[a][:], words[a][:].bitcast(U32).indirect(offsets[:]))

        def gather_scales():
            nc.vector.tensor_copy(picked_scales[:], planes[:].bitcast(U8).indirect(offsets[:]))

        banks = {}
        for m in range(4):
            halves = [(0, 512)] if m < 2 else [(0, 256), (256, 256)]
            banks[m] = [(j0, jn, psum.tile([P, 512], F32, name="acc%d_%d" % (m, j0))) for j0, jn in halves]

        def multiply(u, part, m):
            a, c, n = units[u]
            cols = slice(m * P - c, m * P - c + P)
            for j0, jn, acc in banks[m]:
                nc.tensor.matmul_mx(
                    out=acc[:, 0:jn],
                    lhsT=codes[u][:, part, cols].bitcast(FP8X4),
                    lhsT_scale=scales[u][:, part, cols],
                    rhs=picked[a][:, j0 : j0 + jn].bitcast(FP8X4),
                    rhs_scale=picked_scales[4 * a : P, j0 : j0 + jn],
                    start=(a == 0 and part == 0),
                    stop=(a == 1 and part == 1),
                )

        def finish(m, h, engine):
            j0, jn, acc = banks[m][h]
            res = keep.tile([P, jn], F32, name="res%d_%d" % (m, j0), align_bytes=64)
            if engine == "scalar":
                nc.scalar.activation(res[:], acc[:, 0:jn], ACT.Identity, bias=bias[:, m : m + 1])
            else:
                nc.vector.tensor_scalar(res[:], acc[:, 0:jn], bias[:, m : m + 1], None, op0=ALU.add)
            nc.sync.dma_start(out=out[m * P : (m + 1) * P, j0 : j0 + jn], in_=res[:])

        load_table(0)
        load_offsets()
        load_table(1)
        load_rows()
        load_w(0)
        load_w(1)
        load_w(2)
        load_w(3)
        load_bias()
        take_top(0, 0, 128)
        take_top(0, 128, 128)
        take_top(1, 0, 128)
        take_top(1, 128, 128)
        take_top(2, 0, 256)
        take_top(3, 0, 256)
        gather_words(0)
        gather_words(1)
        gather_scales()
        mask(0, 0, 256)
        rest(0, 0, 256)
        mask(1, 0, 256)
        quantize_both(0)
        multiply(0, 0, 0)
        multiply(0, 1, 0)
        multiply(0, 0, 1)
        multiply(0, 1, 1)
        rest(1, 0, 256)
        mask(2, 0, 256)
        quantize_both(1)
        multiply(1, 0, 0)
        multiply(1, 1, 0)
        finish(0, 0, "scalar")
        multiply(1, 0, 1)
        multiply(1, 1, 1)
        finish(1, 0, "scalar")
        rest(2, 0, 256)
        mask(3, 0, 256)
        quantize_both(2)
        multiply(2, 0, 2)
        multiply(2, 1, 2)
        multiply(2, 0, 3)
        multiply(2, 1, 3)
        rest(3, 0, 128)
        quantize_part(3, 0, 0, 256)
        multiply(3, 0, 2)
        multiply(3, 0, 3)
        rest(3, 128, 128)
        quantize_part(3, 1, 0, 128)
        multiply(3, 1, 2)
        quantize_part(3, 1, 128, 128)
        multiply(3, 1, 3)
        finish(2, 0, "vector")
        finish(2, 1, "scalar")
        finish(3, 0, "vector")
        finish(3, 1, "scalar")
